import numpy as np
import ml_dtypes


def mxq(x, axis, fmt="e4m3"):
    dtype, down = {"e4m3": (ml_dtypes.float8_e4m3fn, 7), "e5m2": (ml_dtypes.float8_e5m2, 14)}[fmt]
    v = np.moveaxis(np.asarray(x, np.float32).astype(ml_dtypes.bfloat16).astype(np.float64), axis, -1)
    blocks = v.reshape(v.shape[:-1] + (-1, 32))
    amax = np.abs(blocks).max(-1, keepdims=True)
    byte = np.maximum(np.where(amax > 0, np.frexp(amax)[1] - 1 + 127, 0) - down, 1)
    scale = np.exp2(byte - 127.0)
    codes = (blocks / scale).astype(np.float32).astype(dtype).astype(np.float64)
    return np.moveaxis((codes * scale).reshape(v.shape), -1, axis)


WIDE = False


def mx_kscale(k):
    if not WIDE:
        return np.ones(k)
    levels = np.array([10, -10, 5, -5, 0])
    if k % 512:
        return np.exp2(np.random.permutation(np.resize(levels, k // 32))).repeat(32)
    a = np.empty((k // 512, 16))
    for p in range(k // 512):
        a[p, :8] = np.random.permutation(np.resize(levels, 8))
        for g in range(8):
            far = levels[np.abs(levels - a[p, g]) >= 10]
            a[p, g + 8] = far[np.random.randint(len(far))]
    return np.exp2(a.ravel()).repeat(32)


def f64(x):
    return np.asarray(x).astype(np.float64)


def striped8(idx):
    return np.asarray(idx).reshape(8, -1, 16).transpose(0, 2, 1).reshape(128, -1).astype(np.uint16)


def unstriped8(offs):
    return offs.reshape(8, 16, -1).transpose(0, 2, 1).reshape(8, -1).astype(np.int64)


def pick8(x, idx, run):
    r = np.arange(len(x))
    return x[r[:, None], idx[r % (8 * run) // run]]


E2M1 = np.array([0.0, 0.5, 1.0, 1.5, 2.0, 3.0, 4.0, 6.0, -0.0, -0.5, -1.0, -1.5, -2.0, -3.0, -4.0, -6.0])


def pack_weight(w, fmt):
    k, n = w.shape
    w = f64(np.asarray(w, np.float32).astype(ml_dtypes.bfloat16)).reshape(k // 32, 32, n)
    amax = np.abs(w).max(1)
    if fmt == "e4m3":
        byte = np.frexp(amax)[1] - 1 + 127 - 7
    else:
        mant, ex = np.frexp(amax / 6.0)
        byte = np.where(mant > 0.5, ex, ex - 1) + 127
    byte = np.clip(np.where(amax > 0, byte, 1), 1, 254)
    scaled = (w * np.exp2(127.0 - byte)[:, None, :]).reshape(k, n).astype(np.float32)
    by_word = np.ascontiguousarray(scaled.reshape(k // 512, 128, 4, n).transpose(0, 1, 3, 2))
    if fmt == "e4m3":
        words = by_word.astype(ml_dtypes.float8_e4m3fn).view(np.uint8)
    else:
        c = by_word.astype(ml_dtypes.float4_e2m1fn).view(np.uint8) & 0xF
        words = (c[..., 0::2] | (c[..., 1::2] << 4)).reshape(k // 512, 128, 2 * n)
    return np.ascontiguousarray(words), np.ascontiguousarray(byte.astype(np.uint8).reshape(k // 512, 16, n))


def unpack_weight(words, scales, fmt):
    g, _, n = scales.shape
    words = np.ascontiguousarray(words).reshape(g, 128, n, -1)
    if fmt == "e4m3":
        vals = words.view(ml_dtypes.float8_e4m3fn).astype(np.float64)
    else:
        nib = np.empty((g, 128, n, 4), np.uint8)
        nib[..., 0::2] = words & 0xF
        nib[..., 1::2] = words >> 4
        vals = E2M1[nib]
    vals = vals * np.repeat(np.exp2(scales.astype(np.float64) - 127.0), 8, axis=1)[..., None]
    return vals.transpose(0, 1, 3, 2).reshape(g * 512, n)


D, T, U, I, Q, E = 512, 1024, 1024, 512, 512, 256


def setup_inputs():
    n = np.random.standard_normal
    idx = np.stack([np.random.permutation(T)[:I] for _ in range(8)])
    idx2 = np.stack([np.random.permutation(U)[:I] for _ in range(8)])
    idx3 = np.stack([np.random.permutation(T)[:I] for _ in range(8)])
    idx4 = np.stack([np.random.permutation(U)[:I] for _ in range(8)])
    idx5 = np.stack([np.random.permutation(T)[:I] for _ in range(8)])
    idx6 = np.stack([np.random.permutation(T)[:I] for _ in range(8)])
    fd = mx_kscale(D)
    fq = mx_kscale(Q)
    keysp = pack_weight(n((D, T)) / fd[:, None], "e2m1")
    notesp = pack_weight(n((D, U)) / fd[:, None], "e4m3")
    mixp = pack_weight(n((Q, E)) * 1.0 / np.sqrt(Q) / fq[:, None], "e4m3")
    return {
        "query": (n((D, Q)) * 1.0 / np.sqrt(D) * fd[:, None]).astype(np.float32),
        "query2": (n((D, Q)) * 1.0 / np.sqrt(D) * fd[:, None]).astype(np.float32),
        "keys_words": keysp[0],
        "keys_scales": keysp[1],
        "notes_words": notesp[0],
        "notes_scales": notesp[1],
        "rowf": (np.random.uniform(0.5, 2.0, (Q, 1)) * fq[:, None]).astype(np.float32),
        "mix_words": mixp[0],
        "mix_scales": mixp[1],
        "offs": striped8(idx),
        "offs2": striped8(idx2),
        "offs3": striped8(idx3),
        "offs4": striped8(idx4),
        "offs5": striped8(idx5),
        "offs6": striped8(idx6),
    }


def reference(query, query2, keys_words, keys_scales, notes_words, notes_scales, rowf, mix_words, mix_scales, offs, offs2, offs3, offs4, offs5, offs6):
    idx = unstriped8(offs)
    idx2 = unstriped8(offs2)
    idx3 = unstriped8(offs3)
    idx4 = unstriped8(offs4)
    idx5 = unstriped8(offs5)
    idx6 = unstriped8(offs6)
    keysu = unpack_weight(keys_words, keys_scales, "e2m1")
    notesu = unpack_weight(notes_words, notes_scales, "e4m3")
    mixu = unpack_weight(mix_words, mix_scales, "e4m3")
    queryq = mxq(f64(query), 0, "e4m3")
    a = queryq.T @ keysu
    query2q = mxq(f64(query2), 0, "e4m3")
    b = query2q.T @ notesu
    w = np.maximum(pick8(a, idx, 64), pick8(b, idx2, 64))
    v = np.maximum(pick8(a, idx3, 64), pick8(b, idx4, 64))
    r = w - v
    f1 = np.zeros((Q, T))
    f1[np.arange(Q)[:, None], idx5[np.arange(Q) % 512 // 64]] = r
    cc = a - f1
    g = pick8(cc, idx6, 64)
    gw = g * f64(rowf)
    gwq = mxq(gw, 0, "e4m3")
    y = mixu.T @ gwq
    return y

@@ -1,0 +1,210 @@
+from contextlib import ExitStack
+
+import concourse.mybir as mybir
+
+D, T, U, I, Q, E = 512, 1024, 1024, 512, 512, 256
+FLOPS = 2 * D * Q * (T + U) + 2 * Q * E * I
+
+F32 = mybir.dt.float32
+BF16 = mybir.dt.bfloat16
+I32 = mybir.dt.int32
+U32 = mybir.dt.uint32
+U16 = mybir.dt.uint16
+U8 = mybir.dt.uint8
+FP8X4 = mybir.dt.float8_e4m3fn_x4
+FP4X4 = mybir.dt.float4_e2m1fn_x4
+ALU = mybir.AluOpType
+COPY = mybir.ActivationFunctionType.Copy
+
+P = 128
+PACK = 4
+BANK = 512
+
+
+def tile_attend_teams_twoq_mixed_kernel(tc, query, query2, keys_words, keys_scales, notes_words, notes_scales, rowf,
+                                         mix_words, mix_scales, offs, offs2, offs3, offs4, offs5, offs6, out):
+    nc = tc.nc
+    with ExitStack() as ctx:
+        held = ctx.enter_context(tc.tile_pool(name="held", bufs=1))
+        psum = ctx.enter_context(tc.psum_pool(name="psum", bufs=8))
+
+        def sb(name, shape, dtype):
+            return held.tile(shape, dtype, name=name, align_bytes=64)
+
+        lists = [sb("list%d" % n, [P, I // 16], U16) for n in range(6)]
+        list_src = [offs, offs2, offs3, offs4, offs5, offs6]
+
+        def load_list(n):
+            nc.sync.dma_start(lists[n][:], list_src[n])
+
+        def load_plane(engine, plane, scales):
+            for quad in range(4):
+                engine.dma_start(plane[32 * quad : 32 * quad + 4, :].bitcast(I32),
+                                 scales[0, 4 * quad : 4 * quad + 4, :].bitcast(I32))
+
+        key_plane = sb("key_plane", [P, T], U8)
+        note_plane = sb("note_plane", [P, U], U8)
+        mix_plane = sb("mix_plane", [P, E], U8)
+        f1 = sb("f1", [P, T], F32)
+        nc.gpsimd.memset(f1[:], 0.0)
+
+        key_words = sb("key_words", [P, 2 * T], U8)
+        note_words = [sb("note_words%d" % n, [P, BANK], U32) for n in range(2)]
+        mix_codes = sb("mix_codes", [P, E], U32)
+        factor = sb("factor", [P, PACK], F32)
+        half = Q // 2
+        raw = [[sb("raw%d_%d" % (s, h), [P, PACK, half], F32) for h in range(2)] for s in range(2)]
+
+        def load_query(s, h):
+            src = (query, query2)[s].rearrange("(p j) q -> p j q", j=PACK)
+            nc.sync.dma_start(raw[s][h][:], src[:, :, h * half : (h + 1) * half])
+
+        notes_flat = notes_words[0].rearrange("p n r -> p (n r)").bitcast(I32)
+        load_query(0, 0)
+        load_query(0, 1)
+        nc.sync.dma_start(key_words[:].bitcast(I32), keys_words[0].bitcast(I32))
+        load_plane(nc.sync, key_plane, keys_scales)
+        load_query(1, 0)
+        load_query(1, 1)
+        load_list(0)
+        load_list(2)
+        load_plane(nc.sync, note_plane, notes_scales)
+        for n in range(2):
+            nc.sync.dma_start(note_words[n][:].bitcast(I32), notes_flat[:, n * BANK : (n + 1) * BANK])
+        for n in (1, 3, 4, 5):
+            load_list(n)
+        nc.sync.dma_start(factor[:], rowf.rearrange("(p t) o -> p (t o)", t=PACK))
+        nc.sync.dma_start(mix_codes[:].bitcast(I32), mix_words[0].rearrange("p n r -> p (n r)").bitcast(I32))
+        load_plane(nc.sync, mix_plane, mix_scales)
+
+        dealt = [sb("dealt%d" % s, [P, PACK, P, PACK], BF16) for s in range(2)]
+        q_codes = [sb("q_codes%d" % s, [P, Q], U32) for s in range(2)]
+        q_plane = [sb("q_plane%d" % s, [P, Q], U8) for s in range(2)]
+
+        def deal(s, h):
+            m = slice(h * half // PACK, (h + 1) * half // PACK)
+            nc.vector.tensor_copy(dealt[s][:, :, m, :].rearrange("p t m j -> p m t j"),
+                                  raw[s][h][:].rearrange("p j (m t) -> p m t j", t=PACK))
+
+        def quantise_query(s, t0, t1):
+            cols = slice(t0 * P, t1 * P)
+            nc.vector.quantize_mx(out=q_codes[s][:, cols].bitcast(FP8X4), scales=q_plane[s][:, cols],
+                                  in_=dealt[s][:, t0:t1, :, :].rearrange("p t m j -> p (t m j)"))
+
+        scores = [[sb("scores%d_%d" % (s, t), [P, T], F32) for t in range(PACK)] for s in range(2)]
+
+        def score(s, t, engines):
+            rows = slice(t * P, (t + 1) * P)
+            for n in range(2):
+                cols = slice(n * BANK, (n + 1) * BANK)
+                bank = psum.tile([P, BANK], F32, name="bank")
+                if s == 0:
+                    moving = key_words[:, 2 * n * BANK : 2 * (n + 1) * BANK].bitcast(FP4X4)
+                    plane = key_plane[:, cols]
+                else:
+                    moving = note_words[n][:].bitcast(FP8X4)
+                    plane = note_plane[:, cols]
+                nc.tensor.matmul_mx(out=bank[:], lhsT=q_codes[s][:, rows].bitcast(FP8X4), lhsT_scale=q_plane[s][:, rows],
+                                    rhs=moving, rhs_scale=plane, start=True, stop=True)
+                if engines[n] == "s":
+                    nc.scalar.copy(scores[s][t][:, cols], bank[:])
+                else:
+                    nc.vector.tensor_copy(scores[s][t][:, cols], bank[:])
+
+        picked = [[sb("picked%d_%d" % (n, t), [P, I], F32) for t in range(PACK)] for n in range(4)]
+
+        def gather(engine, dst, window, offsets, sign=1.0):
+            src = window.indirect(offsets)
+            if engine == "s":
+                nc.scalar.activation(dst, src, COPY, scale=sign)
+            elif sign == 1.0:
+                nc.vector.tensor_copy(dst, src)
+            else:
+                nc.vector.tensor_scalar(dst, src, sign, 0.0, ALU.mult, ALU.add)
+
+        def pick(n, t, engine):
+            gather(engine, picked[n][t][:], scores[n % 2][t][:], lists[n][:], -1.0 if n == 3 else 1.0)
+
+        w = [sb("w%d" % t, [P, I], F32) for t in range(PACK)]
+        neg_v = [sb("neg_v%d" % t, [P, I], F32) for t in range(PACK)]
+        cc = [sb("cc%d" % t, [P, T], F32) for t in range(PACK)]
+        g = sb("g", [P, PACK, I], F32)
+        gw_rows = sb("gw_rows", [P, PACK, I], BF16)
+
+        def teams(t):
+            nc.vector.tensor_tensor(w[t][:], picked[0][t][:], picked[1][t][:], ALU.max)
+            nc.vector.scalar_tensor_tensor(neg_v[t][:], picked[2][t][:], -1.0, picked[3][t][:], ALU.mult, ALU.min)
+
+        def scatter(t):
+            nc.vector.tensor_tensor(f1[:].indirect(lists[4][:]), w[t][:], neg_v[t][:], ALU.add)
+
+        def take_off(t):
+            nc.vector.tensor_tensor(cc[t][:], scores[0][t][:], f1[:], ALU.subtract)
+
+        def left(t, engine, slots):
+            gather(engine, g[:, t, slots], cc[t][:], lists[5][:, slots.start // 16 : slots.stop // 16])
+
+        def weigh(t, engine, slots):
+            if engine == "s":
+                nc.scalar.activation(gw_rows[:, t, slots], g[:, t, slots], COPY, scale=factor[:, t : t + 1])
+            else:
+                nc.vector.tensor_scalar(gw_rows[:, t, slots], g[:, t, slots], factor[:, t : t + 1], None, ALU.mult)
+
+        whole = slice(0, I)
+        halves = [slice(0, I // 2), slice(I // 2, I)]
+
+        deal(0, 0)
+        deal(0, 1)
+        quantise_query(0, 0, 1)
+        quantise_query(0, 1, 4)
+        score(0, 0, "ss")
+        deal(1, 0)
+        deal(1, 1)
+        pick(0, 0, "s")
+        pick(2, 0, "s")
+        quantise_query(1, 0, 1)
+        quantise_query(1, 1, 4)
+        score(1, 0, "vv")
+        pick(1, 0, "s")
+        pick(3, 0, "v")
+        teams(0)
+        scatter(0)
+        for t in range(1, PACK):
+            score(0, t, "ss")
+            score(1, t, "ss")
+            pick(0, t, "s")
+            pick(1, t, "s")
+            pick(3, t, "s")
+            take_off(t - 1)
+            pick(2, t, "v" if t < 3 else "s")
+            teams(t)
+            scatter(t)
+        for t in range(3):
+            left(t, "s", whole)
+            weigh(t, "s", whole)
+        take_off(3)
+        left(3, "v", halves[0])
+        left(3, "s", halves[1])
+        weigh(3, "v", halves[0])
+        weigh(3, "s", halves[1])
+
+        gw = [sb("gw%d" % h, [P, I // 2, PACK], BF16) for h in range(2)]
+        gw_codes = [sb("gw_codes%d" % h, [P, I // 2], U32) for h in range(2)]
+        gw_plane = [sb("gw_plane%d" % h, [P, I // 2], U8) for h in range(2)]
+        for h in range(2):
+            nc.vector.tensor_copy(gw[h][:], gw_rows[:, :, halves[h]].rearrange("p t i -> p i t"))
+        for h in range(2):
+            nc.vector.quantize_mx(out=gw_codes[h][:].bitcast(FP8X4), scales=gw_plane[h][:],
+                                  in_=gw[h][:].rearrange("p i t -> p (i t)"))
+        for h in range(2):
+            for c in range(E // P):
+                chans = slice(c * P, (c + 1) * P)
+                bank = psum.tile([P, I // 2], F32, name="bank")
+                nc.tensor.matmul_mx(out=bank[:], lhsT=mix_codes[:, chans].bitcast(FP8X4), lhsT_scale=mix_plane[:, chans],
+                                    rhs=gw_codes[h][:].bitcast(FP8X4), rhs_scale=gw_plane[h][:], start=True, stop=True)
+                y = sb("y%d_%d" % (h, c), [P, I // 2], F32)
+                if c == 0:
+                    nc.scalar.copy(y[:], bank[:])
+                else:
+                    nc.vector.tensor_copy(y[:], bank[:])
+                nc.sync.dma_start(out[chans, halves[h]], y[:])

@@ -26,10 +26,10 @@ def tile_attend_teams_twoq_mixed_kernel(tc, query, query2, keys_words, keys_scal
     nc = tc.nc
     with ExitStack() as ctx:
         held = ctx.enter_context(tc.tile_pool(name="held", bufs=1))
-        psum = ctx.enter_context(tc.psum_pool(name="psum", bufs=8))
+        psum = ctx.enter_context(tc.psum_pool(name="psum", bufs=6))
 
-        def sb(name, shape, dtype):
-            return held.tile(shape, dtype, name=name, align_bytes=64)
+        def sb(name, shape, dtype, tag=None):
+            return held.tile(shape, dtype, name=name, tag=tag or name, align_bytes=64)
 
         lists = [sb("list%d" % n, [P, I // 16], U16) for n in range(6)]
         list_src = [offs, offs2, offs3, offs4, offs5, offs6]
@@ -45,11 +45,12 @@ def tile_attend_teams_twoq_mixed_kernel(tc, query, query2, keys_words, keys_scal
         key_plane = sb("key_plane", [P, T], U8)
         note_plane = sb("note_plane", [P, U], U8)
         mix_plane = sb("mix_plane", [P, E], U8)
-        f1 = sb("f1", [P, T], F32)
-        nc.gpsimd.memset(f1[:], 0.0)
+        f1 = [sb("f1_%d" % n, [P, T], F32) for n in range(2)]
+        for n in range(2):
+            nc.gpsimd.memset(f1[n][:], 0.0)
 
         key_words = sb("key_words", [P, 2 * T], U8)
-        note_words = [sb("note_words%d" % n, [P, BANK], U32) for n in range(2)]
+        note_words = sb("note_words", [P, U], U32)
         mix_codes = sb("mix_codes", [P, E], U32)
         factor = sb("factor", [P, PACK], F32)
         half = Q // 2
@@ -68,9 +69,8 @@ def tile_attend_teams_twoq_mixed_kernel(tc, query, query2, keys_words, keys_scal
         load_query(1, 1)
         load_list(0)
         load_list(2)
+        nc.sync.dma_start(note_words[:].bitcast(I32), notes_flat)
         load_plane(nc.sync, note_plane, notes_scales)
-        for n in range(2):
-            nc.sync.dma_start(note_words[n][:].bitcast(I32), notes_flat[:, n * BANK : (n + 1) * BANK])
         for n in (1, 3, 4, 5):
             load_list(n)
         nc.sync.dma_start(factor[:], rowf.rearrange("(p t) o -> p (t o)", t=PACK))
@@ -81,20 +81,24 @@ def tile_attend_teams_twoq_mixed_kernel(tc, query, query2, keys_words, keys_scal
         q_codes = [sb("q_codes%d" % s, [P, Q], U32) for s in range(2)]
         q_plane = [sb("q_plane%d" % s, [P, Q], U8) for s in range(2)]
 
-        def deal(s, h):
-            m = slice(h * half // PACK, (h + 1) * half // PACK)
-            nc.vector.tensor_copy(dealt[s][:, :, m, :].rearrange("p t m j -> p m t j"),
-                                  raw[s][h][:].rearrange("p j (m t) -> p m t j", t=PACK))
+        def deal(s, h, share=0):
+            rows = half // PACK
+            dst = dealt[s][:, :, h * rows : (h + 1) * rows, :].rearrange("p t m j -> p m t j")
+            src = raw[s][h][:].rearrange("p j (m t) -> p m t j", t=PACK)
+            nc.vector.tensor_copy(dst[:, share:], src[:, share:])
+            if share:
+                nc.scalar.copy(dst[:, :share], src[:, :share])
 
         def quantise_query(s, t0, t1):
             cols = slice(t0 * P, t1 * P)
             nc.vector.quantize_mx(out=q_codes[s][:, cols].bitcast(FP8X4), scales=q_plane[s][:, cols],
                                   in_=dealt[s][:, t0:t1, :, :].rearrange("p t m j -> p (t m j)"))
 
-        scores = [[sb("scores%d_%d" % (s, t), [P, T], F32) for t in range(PACK)] for s in range(2)]
+        scores = [{}, {}]
 
         def score(s, t, engines):
             rows = slice(t * P, (t + 1) * P)
+            scores[s][t] = sb("scores%d_%d" % (s, t), [P, T], F32, "b%d" % max(t, 1) if s == 1 else None)
             for n in range(2):
                 cols = slice(n * BANK, (n + 1) * BANK)
                 bank = psum.tile([P, BANK], F32, name="bank")
@@ -102,7 +106,7 @@ def tile_attend_teams_twoq_mixed_kernel(tc, query, query2, keys_words, keys_scal
                     moving = key_words[:, 2 * n * BANK : 2 * (n + 1) * BANK].bitcast(FP4X4)
                     plane = key_plane[:, cols]
                 else:
-                    moving = note_words[n][:].bitcast(FP8X4)
+                    moving = note_words[:, cols].bitcast(FP8X4)
                     plane = note_plane[:, cols]
                 nc.tensor.matmul_mx(out=bank[:], lhsT=q_codes[s][:, rows].bitcast(FP8X4), lhsT_scale=q_plane[s][:, rows],
                                     rhs=moving, rhs_scale=plane, start=True, stop=True)
@@ -111,7 +115,7 @@ def tile_attend_teams_twoq_mixed_kernel(tc, query, query2, keys_words, keys_scal
                 else:
                     nc.vector.tensor_copy(scores[s][t][:, cols], bank[:])
 
-        picked = [[sb("picked%d_%d" % (n, t), [P, I], F32) for t in range(PACK)] for n in range(4)]
+        picked = {}
 
         def gather(engine, dst, window, offsets, sign=1.0):
             src = window.indirect(offsets)
@@ -122,39 +126,48 @@ def tile_attend_teams_twoq_mixed_kernel(tc, query, query2, keys_words, keys_scal
             else:
                 nc.vector.tensor_scalar(dst, src, sign, 0.0, ALU.mult, ALU.add)
 
-        def pick(n, t, engine):
-            gather(engine, picked[n][t][:], scores[n % 2][t][:], lists[n][:], -1.0 if n == 3 else 1.0)
+        def pick(n, t, engine, tag=None):
+            picked[n, t] = sb("picked%d_%d" % (n, t), [P, I], F32, tag)
+            gather(engine, picked[n, t][:], scores[n % 2][t][:], lists[n][:], -1.0 if n == 3 else 1.0)
 
-        w = [sb("w%d" % t, [P, I], F32) for t in range(PACK)]
-        neg_v = [sb("neg_v%d" % t, [P, I], F32) for t in range(PACK)]
-        cc = [sb("cc%d" % t, [P, T], F32) for t in range(PACK)]
-        g = sb("g", [P, PACK, I], F32)
-        gw_rows = sb("gw_rows", [P, PACK, I], BF16)
+        w = {}
+        neg_v = {}
+        cc = {}
+        g = {}
+        gw_rows = sb("gw_rows", [P, PACK - 1, I], BF16)
 
-        def teams(t):
-            nc.vector.tensor_tensor(w[t][:], picked[0][t][:], picked[1][t][:], ALU.max)
-            nc.vector.scalar_tensor_tensor(neg_v[t][:], picked[2][t][:], -1.0, picked[3][t][:], ALU.mult, ALU.min)
+        def first_team(t):
+            w[t] = sb("w%d" % t, [P, I], F32)
+            nc.vector.tensor_tensor(w[t][:], picked[0, t][:], picked[1, t][:], ALU.max)
+
+        def second_team(t):
+            neg_v[t] = sb("neg_v%d" % t, [P, I], F32)
+            nc.vector.scalar_tensor_tensor(neg_v[t][:], picked[2, t][:], -1.0, picked[3, t][:], ALU.mult, ALU.min)
 
         def scatter(t):
-            nc.vector.tensor_tensor(f1[:].indirect(lists[4][:]), w[t][:], neg_v[t][:], ALU.add)
+            nc.vector.tensor_tensor(f1[t % 2][:].indirect(lists[4][:]), w[t][:], neg_v[t][:], ALU.add)
 
-        def take_off(t):
-            nc.vector.tensor_tensor(cc[t][:], scores[0][t][:], f1[:], ALU.subtract)
+        def take_off(t, split):
+            cc[t] = sb("cc%d" % t, [P, T], F32, "b%d" % (t + 1))
+            if split:
+                nc.gpsimd.tensor_tensor(cc[t][:, :split], scores[0][t][:, :split], f1[t % 2][:, :split], ALU.subtract)
+            nc.vector.tensor_tensor(cc[t][:, split:], scores[0][t][:, split:], f1[t % 2][:, split:], ALU.subtract)
 
-        def left(t, engine, slots):
-            gather(engine, g[:, t, slots], cc[t][:], lists[5][:, slots.start // 16 : slots.stop // 16])
+        def left(t, engine, slots, tag=None):
+            g[t, slots.start] = sb("g%d_%d" % (t, slots.start), [P, slots.stop - slots.start], F32, tag)
+            gather(engine, g[t, slots.start][:], cc[t][:], lists[5][:, slots.start // 16 : slots.stop // 16])
 
         def weigh(t, engine, slots):
             if engine == "s":
-                nc.scalar.activation(gw_rows[:, t, slots], g[:, t, slots], COPY, scale=factor[:, t : t + 1])
+                nc.scalar.activation(gw_rows[:, t, slots], g[t, slots.start][:], COPY, scale=factor[:, t : t + 1])
             else:
-                nc.vector.tensor_scalar(gw_rows[:, t, slots], g[:, t, slots], factor[:, t : t + 1], None, ALU.mult)
+                nc.vector.tensor_scalar(gw_rows[:, t, slots], g[t, slots.start][:], factor[:, t : t + 1], None, ALU.mult)
 
         whole = slice(0, I)
         halves = [slice(0, I // 2), slice(I // 2, I)]
 
         deal(0, 0)
-        deal(0, 1)
+        deal(0, 1, 20)
         quantise_query(0, 0, 1)
         quantise_query(0, 1, 4)
         score(0, 0, "ss")
@@ -167,32 +180,38 @@ def tile_attend_teams_twoq_mixed_kernel(tc, query, query2, keys_words, keys_scal
         score(1, 0, "vv")
         pick(1, 0, "s")
         pick(3, 0, "v")
-        teams(0)
-        scatter(0)
-        for t in range(1, PACK):
-            score(0, t, "ss")
-            score(1, t, "ss")
-            pick(0, t, "s")
-            pick(1, t, "s")
-            pick(3, t, "s")
-            take_off(t - 1)
-            pick(2, t, "v" if t < 3 else "s")
-            teams(t)
+        second_team(0)
+        first_team(0)
+        for t in range(PACK):
+            if t + 1 < PACK:
+                score(0, t + 1, "ss")
+                if t + 1 in (1, 2):
+                    pick(2, t + 1, "v", "picked2_0")
             scatter(t)
-        for t in range(3):
-            left(t, "s", whole)
-            weigh(t, "s", whole)
-        take_off(3)
-        left(3, "v", halves[0])
-        left(3, "s", halves[1])
-        weigh(3, "v", halves[0])
-        weigh(3, "s", halves[1])
-
+            if t + 1 < PACK:
+                score(1, t + 1, "ss")
+                pick(0, t + 1, "s", "picked1_0" if t == 0 else None)
+                if t + 1 not in (1, 2):
+                    pick(2, t + 1, "s")
+                pick(1, t + 1, "s")
+                pick(3, t + 1, "s")
+                first_team(t + 1)
+                second_team(t + 1)
+                take_off(t, 0)
+        for t in range(PACK - 1):
+            left(t, "s", whole, "left" if t == 2 else None)
+            weigh(t, "v" if t in (0,) else "s", whole)
         gw = [sb("gw%d" % h, [P, I // 2, PACK], BF16) for h in range(2)]
+        last = PACK - 1
+        take_off(last, 0)
+        nc.vector.tensor_copy(gw[0][:, :, :last], gw_rows[:, :, halves[0]].rearrange("p t i -> p i t"))
+        nc.scalar.copy(gw[1][:, :, :last], gw_rows[:, :, halves[1]].rearrange("p t i -> p i t"))
+        left(last, "v", halves[0])
+        left(last, "s", halves[1])
+        nc.vector.tensor_scalar(gw[0][:, :, last], g[last, 0][:], factor[:, last:], None, ALU.mult)
+        nc.scalar.activation(gw[1][:, :, last], g[last, I // 2][:], COPY, scale=factor[:, last:])
         gw_codes = [sb("gw_codes%d" % h, [P, I // 2], U32) for h in range(2)]
         gw_plane = [sb("gw_plane%d" % h, [P, I // 2], U8) for h in range(2)]
-        for h in range(2):
-            nc.vector.tensor_copy(gw[h][:], gw_rows[:, :, halves[h]].rearrange("p t i -> p i t"))
         for h in range(2):
             nc.vector.quantize_mx(out=gw_codes[h][:].bitcast(FP8X4), scales=gw_plane[h][:],
                                   in_=gw[h][:].rearrange("p i t -> p (i t)"))

@@ -50,15 +50,14 @@ def tile_attend_teams_twoq_mixed_kernel(tc, query, query2, keys_words, keys_scal
             nc.gpsimd.memset(f1[n][:], 0.0)
 
         key_words = sb("key_words", [P, 2 * T], U8)
-        note_words = sb("note_words", [P, U], U32)
+        note_words = [sb("note_words%d" % n, [P, BANK], U32) for n in range(2)]
         mix_codes = sb("mix_codes", [P, E], U32)
         factor = sb("factor", [P, PACK], F32)
-        half = Q // 2
-        raw = [[sb("raw%d_%d" % (s, h), [P, PACK, half], F32) for h in range(2)] for s in range(2)]
+        raw = [[sb("raw%d_%d" % (s, h), [P, 2, Q], F32) for h in range(2)] for s in range(2)]
 
         def load_query(s, h):
             src = (query, query2)[s].rearrange("(p j) q -> p j q", j=PACK)
-            nc.sync.dma_start(raw[s][h][:], src[:, :, h * half : (h + 1) * half])
+            nc.sync.dma_start(raw[s][h][:], src[:, 2 * h : 2 * h + 2, :])
 
         notes_flat = notes_words[0].rearrange("p n r -> p (n r)").bitcast(I32)
         load_query(0, 0)
@@ -66,11 +65,12 @@ def tile_attend_teams_twoq_mixed_kernel(tc, query, query2, keys_words, keys_scal
         nc.sync.dma_start(key_words[:].bitcast(I32), keys_words[0].bitcast(I32))
         load_plane(nc.sync, key_plane, keys_scales)
         load_query(1, 0)
-        load_query(1, 1)
         load_list(0)
+        load_query(1, 1)
         load_list(2)
-        nc.sync.dma_start(note_words[:].bitcast(I32), notes_flat)
+        nc.sync.dma_start(note_words[0][:].bitcast(I32), notes_flat[:, :BANK])
         load_plane(nc.sync, note_plane, notes_scales)
+        nc.sync.dma_start(note_words[1][:].bitcast(I32), notes_flat[:, BANK:])
         for n in (1, 3, 4, 5):
             load_list(n)
         nc.sync.dma_start(factor[:], rowf.rearrange("(p t) o -> p (t o)", t=PACK))
@@ -82,8 +82,7 @@ def tile_attend_teams_twoq_mixed_kernel(tc, query, query2, keys_words, keys_scal
         q_plane = [sb("q_plane%d" % s, [P, Q], U8) for s in range(2)]
 
         def deal(s, h, share=0):
-            rows = half // PACK
-            dst = dealt[s][:, :, h * rows : (h + 1) * rows, :].rearrange("p t m j -> p m t j")
+            dst = dealt[s][:, :, :, 2 * h : 2 * h + 2].rearrange("p t m j -> p m t j")
             src = raw[s][h][:].rearrange("p j (m t) -> p m t j", t=PACK)
             nc.vector.tensor_copy(dst[:, share:], src[:, share:])
             if share:
@@ -106,7 +105,7 @@ def tile_attend_teams_twoq_mixed_kernel(tc, query, query2, keys_words, keys_scal
                     moving = key_words[:, 2 * n * BANK : 2 * (n + 1) * BANK].bitcast(FP4X4)
                     plane = key_plane[:, cols]
                 else:
-                    moving = note_words[:, cols].bitcast(FP8X4)
+                    moving = note_words[n][:].bitcast(FP8X4)
                     plane = note_plane[:, cols]
                 nc.tensor.matmul_mx(out=bank[:], lhsT=q_codes[s][:, rows].bitcast(FP8X4), lhsT_scale=q_plane[s][:, rows],
                                     rhs=moving, rhs_scale=plane, start=True, stop=True)
@@ -167,7 +166,7 @@ def tile_attend_teams_twoq_mixed_kernel(tc, query, query2, keys_words, keys_scal
         halves = [slice(0, I // 2), slice(I // 2, I)]
 
         deal(0, 0)
-        deal(0, 1, 20)
+        deal(0, 1, 40)
         quantise_query(0, 0, 1)
         quantise_query(0, 1, 4)
         score(0, 0, "ss")

from contextlib import ExitStack

import concourse.mybir as mybir

D, T, U, I, Q, E = 512, 1024, 1024, 512, 512, 256
FLOPS = 2 * D * Q * (T + U) + 2 * Q * E * I

F32 = mybir.dt.float32
BF16 = mybir.dt.bfloat16
I32 = mybir.dt.int32
U32 = mybir.dt.uint32
U16 = mybir.dt.uint16
U8 = mybir.dt.uint8
FP8X4 = mybir.dt.float8_e4m3fn_x4
FP4X4 = mybir.dt.float4_e2m1fn_x4
ALU = mybir.AluOpType
COPY = mybir.ActivationFunctionType.Copy

P = 128
PACK = 4
BANK = 512


def tile_attend_teams_twoq_mixed_kernel(tc, query, query2, keys_words, keys_scales, notes_words, notes_scales, rowf,
                                         mix_words, mix_scales, offs, offs2, offs3, offs4, offs5, offs6, out):
    nc = tc.nc
    with ExitStack() as ctx:
        held = ctx.enter_context(tc.tile_pool(name="held", bufs=1))
        psum = ctx.enter_context(tc.psum_pool(name="psum", bufs=6))

        def sb(name, shape, dtype, tag=None):
            return held.tile(shape, dtype, name=name, tag=tag or name, align_bytes=64)

        lists = [sb("list%d" % n, [P, I // 16], U16) for n in range(6)]
        list_src = [offs, offs2, offs3, offs4, offs5, offs6]

        def load_list(n):
            nc.sync.dma_start(lists[n][:], list_src[n])

        def load_plane(engine, plane, scales):
            for quad in range(4):
                engine.dma_start(plane[32 * quad : 32 * quad + 4, :].bitcast(I32),
                                 scales[0, 4 * quad : 4 * quad + 4, :].bitcast(I32))

        key_plane = sb("key_plane", [P, T], U8)
        note_plane = sb("note_plane", [P, U], U8)
        mix_plane = sb("mix_plane", [P, E], U8)
        f1 = [sb("f1_%d" % n, [P, T], F32) for n in range(2)]
        for n in range(2):
            nc.gpsimd.memset(f1[n][:], 0.0)

        key_words = sb("key_words", [P, 2 * T], U8)
        note_words = [sb("note_words%d" % n, [P, BANK], U32) for n in range(2)]
        mix_codes = sb("mix_codes", [P, E], U32)
        factor = sb("factor", [P, PACK], F32)
        raw = [[sb("raw%d_%d" % (s, h), [P, 2, Q], F32) for h in range(2)] for s in range(2)]

        def load_query(s, h):
            src = (query, query2)[s].rearrange("(p j) q -> p j q", j=PACK)
            nc.sync.dma_start(raw[s][h][:], src[:, 2 * h : 2 * h + 2, :])

        notes_flat = notes_words[0].rearrange("p n r -> p (n r)").bitcast(I32)
        load_query(0, 0)
        load_query(0, 1)
        nc.sync.dma_start(key_words[:].bitcast(I32), keys_words[0].bitcast(I32))
        load_plane(nc.sync, key_plane, keys_scales)
        load_query(1, 0)
        load_list(0)
        load_query(1, 1)
        load_list(2)
        nc.sync.dma_start(note_words[0][:].bitcast(I32), notes_flat[:, :BANK])
        load_plane(nc.sync, note_plane, notes_scales)
        nc.sync.dma_start(note_words[1][:].bitcast(I32), notes_flat[:, BANK:])
        for n in (1, 3, 4, 5):
            load_list(n)
        nc.sync.dma_start(factor[:], rowf.rearrange("(p t) o -> p (t o)", t=PACK))
        nc.sync.dma_start(mix_codes[:].bitcast(I32), mix_words[0].rearrange("p n r -> p (n r)").bitcast(I32))
        load_plane(nc.sync, mix_plane, mix_scales)

        dealt = [sb("dealt%d" % s, [P, PACK, P, PACK], BF16) for s in range(2)]
        q_codes = [sb("q_codes%d" % s, [P, Q], U32) for s in range(2)]
        q_plane = [sb("q_plane%d" % s, [P, Q], U8) for s in range(2)]

        def deal(s, h, share=0):
            dst = dealt[s][:, :, :, 2 * h : 2 * h + 2].rearrange("p t m j -> p m t j")
            src = raw[s][h][:].rearrange("p j (m t) -> p m t j", t=PACK)
            nc.vector.tensor_copy(dst[:, share:], src[:, share:])
            if share:
                nc.scalar.copy(dst[:, :share], src[:, :share])

        def quantise_query(s, t0, t1):
            cols = slice(t0 * P, t1 * P)
            nc.vector.quantize_mx(out=q_codes[s][:, cols].bitcast(FP8X4), scales=q_plane[s][:, cols],
                                  in_=dealt[s][:, t0:t1, :, :].rearrange("p t m j -> p (t m j)"))

        scores = [{}, {}]

        def score(s, t, engines):
            rows = slice(t * P, (t + 1) * P)
            scores[s][t] = sb("scores%d_%d" % (s, t), [P, T], F32, "b%d" % max(t, 1) if s == 1 else None)
            for n in range(2):
                cols = slice(n * BANK, (n + 1) * BANK)
                bank = psum.tile([P, BANK], F32, name="bank")
                if s == 0:
                    moving = key_words[:, 2 * n * BANK : 2 * (n + 1) * BANK].bitcast(FP4X4)
                    plane = key_plane[:, cols]
                else:
                    moving = note_words[n][:].bitcast(FP8X4)
                    plane = note_plane[:, cols]
                nc.tensor.matmul_mx(out=bank[:], lhsT=q_codes[s][:, rows].bitcast(FP8X4), lhsT_scale=q_plane[s][:, rows],
                                    rhs=moving, rhs_scale=plane, start=True, stop=True)
                if engines[n] == "s":
                    nc.scalar.copy(scores[s][t][:, cols], bank[:])
                else:
                    nc.vector.tensor_copy(scores[s][t][:, cols], bank[:])

        picked = {}

        def gather(engine, dst, window, offsets, sign=1.0):
            src = window.indirect(offsets)
            if engine == "s":
                nc.scalar.activation(dst, src, COPY, scale=sign)
            elif sign == 1.0:
                nc.vector.tensor_copy(dst, src)
            else:
                nc.vector.tensor_scalar(dst, src, sign, 0.0, ALU.mult, ALU.add)

        def pick(n, t, engine, tag=None):
            picked[n, t] = sb("picked%d_%d" % (n, t), [P, I], F32, tag)
            gather(engine, picked[n, t][:], scores[n % 2][t][:], lists[n][:], -1.0 if n == 3 else 1.0)

        w = {}
        neg_v = {}
        cc = {}
        g = {}
        gw_rows = sb("gw_rows", [P, PACK - 1, I], BF16)

        def first_team(t):
            w[t] = sb("w%d" % t, [P, I], F32)
            nc.vector.tensor_tensor(w[t][:], picked[0, t][:], picked[1, t][:], ALU.max)

        def second_team(t):
            neg_v[t] = sb("neg_v%d" % t, [P, I], F32)
            nc.vector.scalar_tensor_tensor(neg_v[t][:], picked[2, t][:], -1.0, picked[3, t][:], ALU.mult, ALU.min)

        def scatter(t):
            nc.vector.tensor_tensor(f1[t % 2][:].indirect(lists[4][:]), w[t][:], neg_v[t][:], ALU.add)

        def take_off(t, split):
            cc[t] = sb("cc%d" % t, [P, T], F32, "b%d" % (t + 1))
            if split:
                nc.gpsimd.tensor_tensor(cc[t][:, :split], scores[0][t][:, :split], f1[t % 2][:, :split], ALU.subtract)
            nc.vector.tensor_tensor(cc[t][:, split:], scores[0][t][:, split:], f1[t % 2][:, split:], ALU.subtract)

        def left(t, engine, slots, tag=None):
            g[t, slots.start] = sb("g%d_%d" % (t, slots.start), [P, slots.stop - slots.start], F32, tag)
            gather(engine, g[t, slots.start][:], cc[t][:], lists[5][:, slots.start // 16 : slots.stop // 16])

        def weigh(t, engine, slots):
            if engine == "s":
                nc.scalar.activation(gw_rows[:, t, slots], g[t, slots.start][:], COPY, scale=factor[:, t : t + 1])
            else:
                nc.vector.tensor_scalar(gw_rows[:, t, slots], g[t, slots.start][:], factor[:, t : t + 1], None, ALU.mult)

        whole = slice(0, I)
        halves = [slice(0, I // 2), slice(I // 2, I)]

        deal(0, 0)
        deal(0, 1, 40)
        quantise_query(0, 0, 1)
        quantise_query(0, 1, 4)
        score(0, 0, "ss")
        deal(1, 0)
        deal(1, 1)
        pick(0, 0, "s")
        pick(2, 0, "s")
        quantise_query(1, 0, 1)
        quantise_query(1, 1, 4)
        score(1, 0, "vv")
        pick(1, 0, "s")
        pick(3, 0, "v")
        second_team(0)
        first_team(0)
        for t in range(PACK):
            if t + 1 < PACK:
                score(0, t + 1, "ss")
                if t + 1 in (1, 2):
                    pick(2, t + 1, "v", "picked2_0")
            scatter(t)
            if t + 1 < PACK:
                score(1, t + 1, "ss")
                pick(0, t + 1, "s", "picked1_0" if t == 0 else None)
                if t + 1 not in (1, 2):
                    pick(2, t + 1, "s")
                pick(1, t + 1, "s")
                pick(3, t + 1, "s")
                first_team(t + 1)
                second_team(t + 1)
                take_off(t, 0)
        for t in range(PACK - 1):
            left(t, "s", whole, "left" if t == 2 else None)
            weigh(t, "v" if t in (0,) else "s", whole)
        gw = [sb("gw%d" % h, [P, I // 2, PACK], BF16) for h in range(2)]
        last = PACK - 1
        take_off(last, 0)
        nc.vector.tensor_copy(gw[0][:, :, :last], gw_rows[:, :, halves[0]].rearrange("p t i -> p i t"))
        nc.scalar.copy(gw[1][:, :, :last], gw_rows[:, :, halves[1]].rearrange("p t i -> p i t"))
        left(last, "v", halves[0])
        left(last, "s", halves[1])
        nc.vector.tensor_scalar(gw[0][:, :, last], g[last, 0][:], factor[:, last:], None, ALU.mult)
        nc.scalar.activation(gw[1][:, :, last], g[last, I // 2][:], COPY, scale=factor[:, last:])
        gw_codes = [sb("gw_codes%d" % h, [P, I // 2], U32) for h in range(2)]
        gw_plane = [sb("gw_plane%d" % h, [P, I // 2], U8) for h in range(2)]
        for h in range(2):
            nc.vector.quantize_mx(out=gw_codes[h][:].bitcast(FP8X4), scales=gw_plane[h][:],
                                  in_=gw[h][:].rearrange("p i t -> p (i t)"))
        for h in range(2):
            for c in range(E // P):
                chans = slice(c * P, (c + 1) * P)
                bank = psum.tile([P, I // 2], F32, name="bank")
                nc.tensor.matmul_mx(out=bank[:], lhsT=mix_codes[:, chans].bitcast(FP8X4), lhsT_scale=mix_plane[:, chans],
                                    rhs=gw_codes[h][:].bitcast(FP8X4), rhs_scale=gw_plane[h][:], start=True, stop=True)
                y = sb("y%d_%d" % (h, c), [P, I // 2], F32)
                if c == 0:
                    nc.scalar.copy(y[:], bank[:])
                else:
                    nc.vector.tensor_copy(y[:], bank[:])
                nc.sync.dma_start(out[chans, halves[h]], y[:])
